import numpy as np
import ml_dtypes


def mxq(x, axis, fmt="e4m3"):
    dtype, down = {"e4m3": (ml_dtypes.float8_e4m3fn, 7), "e5m2": (ml_dtypes.float8_e5m2, 14)}[fmt]
    v = np.moveaxis(np.asarray(x, np.float32).astype(ml_dtypes.bfloat16).astype(np.float64), axis, -1)
    blocks = v.reshape(v.shape[:-1] + (-1, 32))
    amax = np.abs(blocks).max(-1, keepdims=True)
    byte = np.maximum(np.where(amax > 0, np.frexp(amax)[1] - 1 + 127, 0) - down, 1)
    scale = np.exp2(byte - 127.0)
    codes = (blocks / scale).astype(np.float32).astype(dtype).astype(np.float64)
    return np.moveaxis((codes * scale).reshape(v.shape), -1, axis)


WIDE = False


def mx_kscale(k):
    if not WIDE:
        return np.ones(k)
    levels = np.array([10, -10, 5, -5, 0])
    if k % 512:
        return np.exp2(np.random.permutation(np.resize(levels, k // 32))).repeat(32)
    a = np.empty((k // 512, 16))
    for p in range(k // 512):
        a[p, :8] = np.random.permutation(np.resize(levels, 8))
        for g in range(8):
            far = levels[np.abs(levels - a[p, g]) >= 10]
            a[p, g + 8] = far[np.random.randint(len(far))]
    return np.exp2(a.ravel()).repeat(32)


def f64(x):
    return np.asarray(x).astype(np.float64)


def striped(idx):
    return np.tile(idx.reshape(-1, 16).T, (8, 1)).astype(np.uint16)


def unstriped(offs):
    return offs[:16].T.reshape(-1).astype(np.int64)


E2M1 = np.array([0.0, 0.5, 1.0, 1.5, 2.0, 3.0, 4.0, 6.0, -0.0, -0.5, -1.0, -1.5, -2.0, -3.0, -4.0, -6.0])


def pack_weight(w, fmt):
    k, n = w.shape
    w = f64(np.asarray(w, np.float32).astype(ml_dtypes.bfloat16)).reshape(k // 32, 32, n)
    amax = np.abs(w).max(1)
    if fmt == "e4m3":
        byte = np.frexp(amax)[1] - 1 + 127 - 7
    else:
        mant, ex = np.frexp(amax / 6.0)
        byte = np.where(mant > 0.5, ex, ex - 1) + 127
    byte = np.clip(np.where(amax > 0, byte, 1), 1, 254)
    scaled = (w * np.exp2(127.0 - byte)[:, None, :]).reshape(k, n).astype(np.float32)
    by_word = np.ascontiguousarray(scaled.reshape(k // 512, 128, 4, n).transpose(0, 1, 3, 2))
    if fmt == "e4m3":
        words = by_word.astype(ml_dtypes.float8_e4m3fn).view(np.uint8)
    else:
        c = by_word.astype(ml_dtypes.float4_e2m1fn).view(np.uint8) & 0xF
        words = (c[..., 0::2] | (c[..., 1::2] << 4)).reshape(k // 512, 128, 2 * n)
    return np.ascontiguousarray(words), np.ascontiguousarray(byte.astype(np.uint8).reshape(k // 512, 16, n))


def unpack_weight(words, scales, fmt):
    g, _, n = scales.shape
    words = np.ascontiguousarray(words).reshape(g, 128, n, -1)
    if fmt == "e4m3":
        vals = words.view(ml_dtypes.float8_e4m3fn).astype(np.float64)
    else:
        nib = np.empty((g, 128, n, 4), np.uint8)
        nib[..., 0::2] = words & 0xF
        nib[..., 1::2] = words >> 4
        vals = E2M1[nib]
    vals = vals * np.repeat(np.exp2(scales.astype(np.float64) - 127.0), 8, axis=1)[..., None]
    return vals.transpose(0, 1, 3, 2).reshape(g * 512, n)


def gelu(v):
    return 0.5 * v * (1.0 + np.tanh(np.sqrt(2.0 / np.pi) * (v + 0.044715 * v**3)))


K, H, T, S, T2, P = 1024, 512, 4096, 1024, 2048, 1024


def setup_inputs():
    n = np.random.standard_normal
    s = mx_kscale(K)[:, None]
    u = mx_kscale(H)[:, None]
    d = {}
    d["tab_words"], d["tab_scales"] = pack_weight(n((K, T)) * s, "e4m3")
    d["offs"] = striped(np.random.permutation(T)[:S])
    d["offs2"] = striped(np.random.permutation(T2)[:S])
    d["offs3"] = striped(np.random.permutation(T2)[:P])
    d["offs4"] = striped(np.random.permutation(T2)[:P])
    d["w1"] = (n((K, H)) * 0.7 / K ** 0.5 / s).astype(np.float32)
    d["w4_words"], d["w4_scales"] = pack_weight(-n((K, H)) * 0.7 / K ** 0.5 / s, "e2m1")
    d["gain"] = (0.6 * np.exp(0.3 * n(H)) * np.sign(n(H)) * u[:, 0]).astype(np.float32)
    d["wgs"] = np.exp(0.3 * n((128, S))).astype(np.float32)
    d["page0"] = (n((H, T2)) * u).astype(np.float32)
    d["reach"] = np.random.uniform(0.5, 1.6, H).astype(np.float32)
    d["w2"] = (n((H, H)) / H ** 0.5 / u).astype(np.float32)
    d["w8_words"], d["w8_scales"] = pack_weight(n((H, H)) / H ** 0.5 / u, "e4m3")
    d["mir"] = (np.random.uniform(1.2, 2.5, H) / u[:, 0]).astype(np.float32)
    return d


def reference(tab_words, tab_scales, offs, offs2, offs3, offs4, w1, w4_words, w4_scales, gain, wgs, page0, reach, w2, w8_words, w8_scales, mir):
    v = unpack_weight(tab_words, tab_scales, "e4m3")[:, unstriped(offs)]
    w4 = unpack_weight(w4_words, w4_scales, "e2m1")
    diff = mxq(f64(w1), 0, "e4m3").T @ v + w4.T @ v
    h = f64(gain)[:, None] * np.square(diff)
    page = f64(page0).copy()
    page[:, unstriped(offs2)] = np.tile(f64(wgs), (H // 128, 1)) * h
    x = mxq(page[:, unstriped(offs3)] * f64(reach)[:, None], 0, "e4m3")
    y1 = mxq(f64(w2), 0, "e4m3").T @ x
    y2 = unpack_weight(w8_words, w8_scales, "e4m3").T @ x
    b = page[:, unstriped(offs4)] * f64(mir)[:, None]
    return np.maximum(y1, y2) * (1.0 / (1.0 + np.exp(-b)))

@@ -1,0 +1,264 @@
+from contextlib import ExitStack
+
+import concourse.mybir as mybir
+
+K, H, T, S, T2, M = 1024, 512, 4096, 1024, 2048, 1024
+FLOPS = 2 * (2 * K * H * S + 2 * H * H * M)
+
+F32 = mybir.dt.float32
+BF16 = mybir.dt.bfloat16
+I32 = mybir.dt.int32
+U32 = mybir.dt.uint32
+U16 = mybir.dt.uint16
+U8 = mybir.dt.uint8
+FP8X4 = mybir.dt.float8_e4m3fn_x4
+FP4X4 = mybir.dt.float4_e2m1fn_x4
+ACT = mybir.ActivationFunctionType
+ALU = mybir.AluOpType
+
+P = 128
+PACK = 4
+QUADS = 4
+HALF = 512
+LIST_HALF = HALF // 16
+SPARE = 96
+
+
+def tile_list_inclusion_page_planes_kernel(
+    tc, tab_words, tab_scales, offs, offs2, offs3, offs4, w1, w4_words, w4_scales,
+    gain, wgs, page0, reach, w2, w8_words, w8_scales, mir, out,
+):
+    nc = tc.nc
+    with ExitStack() as ctx:
+        keep = ctx.enter_context(tc.tile_pool(name="keep", bufs=1))
+        ring = ctx.enter_context(tc.tile_pool(name="ring", bufs=2))
+        psum = ctx.enter_context(tc.psum_pool(name="psum", bufs=1))
+
+        def sb(name, shape, dtype, tag=None):
+            return keep.tile(shape, dtype, name=name, tag=tag or name, align_bytes=64)
+
+        def bank(b):
+            return psum.tile([P, HALF], F32, name="bank%d" % b)
+
+        def load_list(name, src):
+            tile = keep.tile([P, S // 16], U16, name=name)
+            nc.sync.dma_start(tile[:], src)
+            return tile
+
+        def load_scale_rows(name, src, width, clear):
+            tile = sb(name, [P, width], U8)
+            clear(tile[0:SPARE, :].bitcast(I32), 0)
+            nc.sync.dma_start(tile[SPARE:P, :].bitcast(I32), src.rearrange("a q c -> q a c").bitcast(I32))
+            return tile
+
+        def load_vector(name, src):
+            tile = sb(name, [P, PACK], F32)
+            nc.sync.dma_start(tile[:], src.rearrange("(p t) -> p t", t=PACK))
+            return tile
+
+        def load_table(a):
+            tile = sb("tab%d" % a, [P, T], I32)
+            nc.sync.dma_start(tile[:], tab_words[a].rearrange("p c i -> p (c i)").bitcast(I32))
+            return tile
+
+        def load_weight_rows(name, rows):
+            tile = sb(name, [P, PACK, H], F32)
+            nc.sync.dma_start(tile[:], rows.rearrange("(p j) c -> p j c", j=PACK))
+            return tile
+
+        wgs_rows = wgs.rearrange("(p t) j -> p (t j)", t=PACK)
+
+        def load_wgs(name, lo, hi):
+            tile = sb(name, [P, hi - lo], F32)
+            for q in (0, 2, 1, 3):
+                nc.sync.dma_start(tile[32 * q : 32 * q + 32, :], wgs_rows[:, lo:hi])
+            return tile
+
+        page_rows = page0.rearrange("(p t) c -> p t c", t=PACK)
+
+        def load_page(t):
+            tile = sb("page%d" % t, [P, T2], F32)
+            nc.sync.dma_start(tile[:], page_rows[:, t, :])
+            return tile
+
+        list1 = load_list("list1", offs)
+        tab_sc = load_scale_rows("tab_sc", tab_scales, T, nc.vector.memset)
+        w4_sc_raw = load_scale_rows("w4_sc_raw", w4_scales, H, nc.vector.memset)
+        planes = sb("planes", [P, 2, S + H], U8)
+        nc.gpsimd.memset(planes[:].bitcast(I32), 0)
+        w8_sc_raw = sb("w8_sc_raw", [P, H], U8)
+        nc.gpsimd.memset(w8_sc_raw[:].bitcast(I32), 0)
+        tab = [load_table(0)]
+        w4_raw = sb("w4_raw", [P, 2, 2 * H], U8)
+        nc.sync.dma_start(w4_raw[:].bitcast(I32), w4_words.rearrange("a p b -> p a b").bitcast(I32))
+        w1_raw = [load_weight_rows("w1_raw%d" % a, w1[512 * a : 512 * (a + 1), :]) for a in range(2)]
+        tab.append(load_table(1))
+        gain_t = load_vector("gain_t", gain)
+        list2 = load_list("list2", offs2)
+        wgs_0a = load_wgs("wgs_0a", 0, HALF)
+        page = [load_page(0)]
+        wgs_0b = load_wgs("wgs_0b", HALF, S)
+        list3 = load_list("list3", offs3)
+        reach_t = load_vector("reach_t", reach)
+        page.append(load_page(1))
+        wgs_1 = load_wgs("wgs_1", S, 2 * S)
+        w2_raw = load_weight_rows("w2_raw", w2)
+        w8_raw = sb("w8_raw", [P, H], I32)
+        nc.sync.dma_start(w8_raw[:], w8_words[0].rearrange("p c i -> p (c i)").bitcast(I32))
+        for q in range(QUADS):
+            nc.sync.dma_start(
+                w8_sc_raw[32 * q : 32 * q + 4, :].bitcast(I32), w8_scales[0, 4 * q : 4 * q + 4, :].bitcast(I32)
+            )
+        page.append(load_page(2))
+        wgs_23 = load_wgs("wgs_23", 2 * S, 4 * S)
+        page.append(load_page(3))
+        list4 = load_list("list4", offs4)
+        mir_t = load_vector("mir_t", mir)
+
+        def quantise_weight(name, raw, tag=None):
+            grouped = sb(name + "_bf", [P, PACK, P, PACK], BF16)
+            nc.scalar.copy(
+                grouped[:].rearrange("p t q j -> p q j t"),
+                raw[:].rearrange("p j (q t) -> p q j t", t=PACK),
+            )
+            codes = sb(name + "_codes", [P, H], U32, tag)
+            scales = sb(name + "_scales", [P, H], U8)
+            nc.vector.quantize_mx(
+                out=codes[:].bitcast(FP8X4), scales=scales[:],
+                in_=grouped[:].rearrange("p t q j -> p (t q j)"),
+            )
+            return codes, scales
+
+        def deal(dst, raw, unit):
+            nc.vector.tensor_copy(
+                dst.rearrange("p (t q b) -> p q t b", t=PACK, b=unit),
+                raw.rearrange("p (q t b) -> p q t b", t=PACK, b=unit),
+            )
+
+        def gather_words(a, h):
+            tile = sb("v_w%d_%d" % (a, h), [P, HALF], U32)
+            nc.vector.tensor_copy(
+                tile[:], tab[a][:].bitcast(U32).indirect(list1[:, LIST_HALF * h : LIST_HALF * (h + 1)])
+            )
+            return tile
+
+        staged = sb("staged", [P, S + H], U8)
+        deal(staged[:, S : S + H], w4_sc_raw[:], 1)
+        picked_sc = sb("picked_sc", [P, S], U8)
+        nc.vector.tensor_copy(picked_sc[:], tab_sc[:].indirect(list1[:]))
+        nc.vector.tensor_copy(staged[:, 0:S].bitcast(I32), picked_sc[:].bitcast(I32))
+        for q in range(QUADS):
+            nc.gpsimd.dma_start(
+                planes[32 * q : 32 * q + 4, :, :].bitcast(I32),
+                staged[SPARE + 8 * q : SPARE + 8 * q + 8, :].bitcast(I32),
+            )
+        v_w = [[gather_words(0, h) for h in range(2)]]
+        w4_codes = [sb("w4_codes%d" % a, [P, 2 * H], U8) for a in range(2)]
+        w1_q = []
+        for a in range(2):
+            deal(w4_codes[a][:], w4_raw[:, a, :], 2)
+            w1_q.append(quantise_weight("w1_%d" % a, w1_raw[a]))
+        v_w.append([gather_words(1, h) for h in range(2)])
+
+        diff = [[bank(2 * t + h) for h in range(2)] for t in range(PACK)]
+
+        def diff_passes(a, t, h):
+            cols = slice(P * t, P * (t + 1))
+            rhs = v_w[a][h][:].bitcast(FP8X4)
+            rhs_scale = planes[:, a, HALF * h : HALF * (h + 1)]
+            nc.tensor.matmul_mx(
+                out=diff[t][h][:],
+                lhsT=w4_codes[a][:, 2 * P * t : 2 * P * (t + 1)].bitcast(FP4X4), lhsT_scale=planes[:, a, S + P * t : S + P * (t + 1)],
+                rhs=rhs, rhs_scale=rhs_scale, start=(a == 0), stop=False,
+            )
+            nc.tensor.matmul_mx(
+                out=diff[t][h][:],
+                lhsT=w1_q[a][0][:, cols].bitcast(FP8X4), lhsT_scale=w1_q[a][1][:, cols],
+                rhs=rhs, rhs_scale=rhs_scale, start=False, stop=(a == 1),
+            )
+
+        work = [sb("work%d" % h, [P, S], F32) for h in range(2)]
+        x_bf = [work[h][:].bitcast(BF16) for h in range(2)]
+        hval = [sb("hval%d" % t, [P, S], F32) for t in range(PACK)]
+        for t in range(PACK):
+            for h in range(2):
+                diff_passes(0, t, h)
+            for h in range(2):
+                diff_passes(1, t, h)
+                part = hval[t][:, HALF * h : HALF * (h + 1)]
+                squared = work[1 - h][:, 0:HALF]
+                nc.scalar.activation(squared, diff[t][h][:], ACT.Square)
+                nc.scalar.activation(part, squared, ACT.Copy, scale=gain_t[:, t : t + 1])
+
+
+        def put(t, entries, values, weights):
+            nc.vector.tensor_tensor(page[t][:].indirect(entries), values, weights, ALU.mult)
+
+        def scale_into_x(t, h, picked):
+            nc.scalar.activation(x_bf[h][:, t : PACK * HALF : PACK], picked, ACT.Copy, scale=reach_t[:, t : t + 1])
+
+        for t in range(PACK):
+            if t == 0:
+                put(0, list2[:, 0:LIST_HALF], hval[0][:, 0:HALF], wgs_0a[:])
+                put(0, list2[:, LIST_HALF : 2 * LIST_HALF], hval[0][:, HALF:S], wgs_0b[:])
+            elif t == 1:
+                put(1, list2[:], hval[1][:], wgs_1[:])
+            else:
+                put(t, list2[:], hval[t][:], wgs_23[:, S * (t - 2) : S * (t - 1)])
+            picked = ring.tile([P, M], F32, name="picked", align_bytes=64)
+            if t < PACK - 1:
+                nc.vector.tensor_copy(picked[:], page[t][:].indirect(list3[:]))
+                for h in range(2):
+                    scale_into_x(t, h, picked[:, HALF * h : HALF * (h + 1)])
+            else:
+                for h in range(2):
+                    part = picked[:, HALF * h : HALF * (h + 1)]
+                    nc.vector.tensor_copy(part, page[t][:].indirect(list3[:, LIST_HALF * h : LIST_HALF * (h + 1)]))
+                    scale_into_x(t, h, part)
+
+        w2_codes, w2_sc = quantise_weight("w2", w2_raw, "hval2")
+        w8_codes = sb("w8_codes", [P, H], I32, "hval1")
+        deal(w8_codes[:], w8_raw[:], 1)
+        w8_sc = sb("w8_sc", [P, H], U8, "wgs_1")
+        deal(w8_sc[:], w8_sc_raw[:], 1)
+
+        x_q = []
+        for h in range(2):
+            codes = sb("x_codes%d" % h, [P, HALF], U32)
+            scales = sb("x_scales%d" % h, [P, HALF], U8)
+            nc.vector.quantize_mx(
+                out=codes[:].bitcast(FP8X4), scales=scales[:], in_=x_bf[h]
+            )
+            x_q.append((codes, scales))
+
+        gate = [hval[0][:], hval[3][:], work[0][:], work[1][:]]
+        for t in range(PACK):
+            nc.vector.tensor_copy(gate[t], page[t][:].indirect(list4[:]))
+            nc.scalar.activation(gate[t], gate[t], ACT.Sigmoid, scale=mir_t[:, t : t + 1])
+
+        out_rows = out.rearrange("(p t) m -> p t m", t=PACK)
+        units = [(h, t) for h in range(2) for t in range(PACK)]
+        larger = []
+
+        def finish(u):
+            h, t = units[u]
+            cols = slice(HALF * h, HALF * (h + 1))
+            nc.vector.tensor_tensor(larger[u][:], larger[u][:], gate[t][:, cols], ALU.mult)
+            nc.sync.dma_start(out_rows[:, t, cols], larger[u][:])
+
+        for u, (h, t) in enumerate(units):
+            cols = slice(P * t, P * (t + 1))
+            y1 = bank((2 * u) % 8)
+            y2 = bank((2 * u + 1) % 8)
+            for y, codes, scales in ((y1, w2_codes, w2_sc), (y2, w8_codes, w8_sc)):
+                nc.tensor.matmul_mx(
+                    out=y[:], lhsT=codes[:, cols].bitcast(FP8X4), lhsT_scale=scales[:, cols],
+                    rhs=x_q[h][0][:].bitcast(FP8X4), rhs_scale=x_q[h][1][:], start=True, stop=True,
+                )
+            side = sb("larger%d" % u, [P, HALF], F32)
+            nc.scalar.copy(side[:], y1[:])
+            nc.vector.tensor_tensor(side[:], y2[:], side[:], ALU.max)
+            larger.append(side)
+            if u > 0:
+                finish(u - 1)
+        finish(len(units) - 1)

@@ -109,11 +109,11 @@ def tile_list_inclusion_page_planes_kernel(
             nc.sync.dma_start(
                 w8_sc_raw[32 * q : 32 * q + 4, :].bitcast(I32), w8_scales[0, 4 * q : 4 * q + 4, :].bitcast(I32)
             )
+        list4 = load_list("list4", offs4)
+        mir_t = load_vector("mir_t", mir)
         page.append(load_page(2))
         wgs_23 = load_wgs("wgs_23", 2 * S, 4 * S)
         page.append(load_page(3))
-        list4 = load_list("list4", offs4)
-        mir_t = load_vector("mir_t", mir)
 
         def quantise_weight(name, raw, tag=None):
             grouped = sb(name + "_bf", [P, PACK, P, PACK], BF16)
@@ -160,19 +160,19 @@ def tile_list_inclusion_page_planes_kernel(
             w1_q.append(quantise_weight("w1_%d" % a, w1_raw[a]))
         v_w.append([gather_words(1, h) for h in range(2)])
 
-        diff = [[bank(2 * t + h) for h in range(2)] for t in range(PACK)]
+        diff = {}
 
         def diff_passes(a, t, h):
             cols = slice(P * t, P * (t + 1))
             rhs = v_w[a][h][:].bitcast(FP8X4)
             rhs_scale = planes[:, a, HALF * h : HALF * (h + 1)]
             nc.tensor.matmul_mx(
-                out=diff[t][h][:],
+                out=diff[t, h][:],
                 lhsT=w4_codes[a][:, 2 * P * t : 2 * P * (t + 1)].bitcast(FP4X4), lhsT_scale=planes[:, a, S + P * t : S + P * (t + 1)],
                 rhs=rhs, rhs_scale=rhs_scale, start=(a == 0), stop=False,
             )
             nc.tensor.matmul_mx(
-                out=diff[t][h][:],
+                out=diff[t, h][:],
                 lhsT=w1_q[a][0][:, cols].bitcast(FP8X4), lhsT_scale=w1_q[a][1][:, cols],
                 rhs=rhs, rhs_scale=rhs_scale, start=False, stop=(a == 1),
             )
@@ -182,12 +182,12 @@ def tile_list_inclusion_page_planes_kernel(
         hval = [sb("hval%d" % t, [P, S], F32) for t in range(PACK)]
         for t in range(PACK):
             for h in range(2):
+                diff[t, h] = bank(h)
                 diff_passes(0, t, h)
-            for h in range(2):
                 diff_passes(1, t, h)
                 part = hval[t][:, HALF * h : HALF * (h + 1)]
                 squared = work[1 - h][:, 0:HALF]
-                nc.scalar.activation(squared, diff[t][h][:], ACT.Square)
+                nc.scalar.activation(squared, diff[t, h][:], ACT.Square)
                 nc.scalar.activation(part, squared, ACT.Copy, scale=gain_t[:, t : t + 1])
 
 
@@ -231,22 +231,17 @@ def tile_list_inclusion_page_planes_kernel(
             )
             x_q.append((codes, scales))
 
-        gate = [hval[0][:], hval[3][:], work[0][:], work[1][:]]
-        for t in range(PACK):
-            nc.vector.tensor_copy(gate[t], page[t][:].indirect(list4[:]))
-            nc.scalar.activation(gate[t], gate[t], ACT.Sigmoid, scale=mir_t[:, t : t + 1])
-
         out_rows = out.rearrange("(p t) m -> p t m", t=PACK)
-        units = [(h, t) for h in range(2) for t in range(PACK)]
-        larger = []
+        units = [(t, h) for h in range(2) for t in range(PACK - 1)] + [(PACK - 1, h) for h in range(2)]
+        first = [sb("first%d" % i, [P, M], F32) for i in range(PACK)]
+        gate = [hval[0], hval[3], work[0], first[0]]
 
-        def finish(u):
-            h, t = units[u]
-            cols = slice(HALF * h, HALF * (h + 1))
-            nc.vector.tensor_tensor(larger[u][:], larger[u][:], gate[t][:, cols], ALU.mult)
-            nc.sync.dma_start(out_rows[:, t, cols], larger[u][:])
+        def mirror(t):
+            nc.vector.tensor_copy(gate[t][:], page[t][:].indirect(list4[:]))
+            nc.scalar.activation(gate[t][:], gate[t][:], ACT.Sigmoid, scale=mir_t[:, t : t + 1])
 
-        for u, (h, t) in enumerate(units):
+        def larger_side(u):
+            t, h = units[u]
             cols = slice(P * t, P * (t + 1))
             y1 = bank((2 * u) % 8)
             y2 = bank((2 * u + 1) % 8)
@@ -255,10 +250,27 @@ def tile_list_inclusion_page_planes_kernel(
                     out=y[:], lhsT=codes[:, cols].bitcast(FP8X4), lhsT_scale=scales[:, cols],
                     rhs=x_q[h][0][:].bitcast(FP8X4), rhs_scale=x_q[h][1][:], start=True, stop=True,
                 )
-            side = sb("larger%d" % u, [P, HALF], F32)
-            nc.scalar.copy(side[:], y1[:])
-            nc.vector.tensor_tensor(side[:], y2[:], side[:], ALU.max)
-            larger.append(side)
-            if u > 0:
-                finish(u - 1)
-        finish(len(units) - 1)
+            side = first[u // 2][:, HALF * (u % 2) : HALF * (u % 2 + 1)]
+            nc.scalar.copy(side, y1[:])
+            larger = sb("larger%d" % u, [P, HALF], F32)
+            nc.vector.tensor_tensor(larger[:], y2[:], side, ALU.max)
+            return larger
+
+        def finish(u, larger):
+            t, h = units[u]
+            cols = slice(HALF * h, HALF * (h + 1))
+            engine = nc.gpsimd if t < PACK - 1 else nc.vector
+            engine.tensor_tensor(larger[:], larger[:], gate[t][:, cols], ALU.mult)
+            nc.sync.dma_start(out_rows[:, t, cols], larger[:])
+
+        for t in range(PACK - 1):
+            mirror(t)
+        larger = []
+        for u in range(len(units)):
+            larger.append(larger_side(u))
+            if u == 2:
+                mirror(PACK - 1)
+            if u < len(units) - 2:
+                finish(u, larger[u])
+        for u in range(len(units) - 2, len(units)):
+            finish(u, larger[u])

@@ -84,43 +84,43 @@ def tile_list_inclusion_page_planes_kernel(
         list1 = load_list("list1", offs)
         tab_sc = load_scale_rows("tab_sc", tab_scales, T, nc.vector.memset)
         w4_sc_raw = load_scale_rows("w4_sc_raw", w4_scales, H, nc.vector.memset)
-        planes = sb("planes", [P, 2, S + H], U8)
+        staged = sb("staged", [P, S + H + H // 2], U8)
+        nc.sync.dma_start(
+            staged[SPARE:P, S + H : S + H + H // 2].bitcast(I32),
+            w8_scales[0].rearrange("q (a c) -> (q a) c", a=2).bitcast(I32),
+        )
+        planes = sb("planes", [P, 2, S + H + H // 2], U8)
         nc.gpsimd.memset(planes[:].bitcast(I32), 0)
-        w8_sc_raw = sb("w8_sc_raw", [P, H], U8)
-        nc.gpsimd.memset(w8_sc_raw[:].bitcast(I32), 0)
         tab = [load_table(0)]
         w4_raw = sb("w4_raw", [P, 2, 2 * H], U8)
         nc.sync.dma_start(w4_raw[:].bitcast(I32), w4_words.rearrange("a p b -> p a b").bitcast(I32))
         w1_raw = [load_weight_rows("w1_raw%d" % a, w1[512 * a : 512 * (a + 1), :]) for a in range(2)]
         tab.append(load_table(1))
         gain_t = load_vector("gain_t", gain)
-        list2 = load_list("list2", offs2)
         wgs_0a = load_wgs("wgs_0a", 0, HALF)
+        w8_raw = sb("w8_raw", [P, H], I32)
+        nc.sync.dma_start(w8_raw[:], w8_words[0].rearrange("p c i -> p (c i)").bitcast(I32))
         page = [load_page(0)]
+        list2 = load_list("list2", offs2)
         wgs_0b = load_wgs("wgs_0b", HALF, S)
         list3 = load_list("list3", offs3)
         reach_t = load_vector("reach_t", reach)
         page.append(load_page(1))
         wgs_1 = load_wgs("wgs_1", S, 2 * S)
         w2_raw = load_weight_rows("w2_raw", w2)
-        w8_raw = sb("w8_raw", [P, H], I32)
-        nc.sync.dma_start(w8_raw[:], w8_words[0].rearrange("p c i -> p (c i)").bitcast(I32))
-        for q in range(QUADS):
-            nc.sync.dma_start(
-                w8_sc_raw[32 * q : 32 * q + 4, :].bitcast(I32), w8_scales[0, 4 * q : 4 * q + 4, :].bitcast(I32)
-            )
         list4 = load_list("list4", offs4)
         mir_t = load_vector("mir_t", mir)
         page.append(load_page(2))
         wgs_23 = load_wgs("wgs_23", 2 * S, 4 * S)
         page.append(load_page(3))
 
-        def quantise_weight(name, raw, tag=None):
+        def quantise_weight(name, raw, scalar_share, tag=None):
             grouped = sb(name + "_bf", [P, PACK, P, PACK], BF16)
-            nc.scalar.copy(
-                grouped[:].rearrange("p t q j -> p q j t"),
-                raw[:].rearrange("p j (q t) -> p q j t", t=PACK),
-            )
+            dst = grouped[:].rearrange("p t q j -> p q t j")
+            src = raw[:].rearrange("p j (q t) -> p q t j", t=PACK)
+            nc.scalar.copy(dst[:, 0:scalar_share], src[:, 0:scalar_share])
+            if scalar_share < P:
+                nc.vector.tensor_copy(dst[:, scalar_share:P], src[:, scalar_share:P])
             codes = sb(name + "_codes", [P, H], U32, tag)
             scales = sb(name + "_scales", [P, H], U8)
             nc.vector.quantize_mx(
@@ -131,8 +131,8 @@ def tile_list_inclusion_page_planes_kernel(
 
         def deal(dst, raw, unit):
             nc.vector.tensor_copy(
-                dst.rearrange("p (t q b) -> p q t b", t=PACK, b=unit),
-                raw.rearrange("p (q t b) -> p q t b", t=PACK, b=unit),
+                dst.rearrange("p (t q b) -> p t q b", t=PACK, b=unit),
+                raw.rearrange("p (q t b) -> p t q b", t=PACK, b=unit),
             )
 
         def gather_words(a, h):
@@ -142,7 +142,6 @@ def tile_list_inclusion_page_planes_kernel(
             )
             return tile
 
-        staged = sb("staged", [P, S + H], U8)
         deal(staged[:, S : S + H], w4_sc_raw[:], 1)
         picked_sc = sb("picked_sc", [P, S], U8)
         nc.vector.tensor_copy(picked_sc[:], tab_sc[:].indirect(list1[:]))
@@ -157,8 +156,15 @@ def tile_list_inclusion_page_planes_kernel(
         w1_q = []
         for a in range(2):
             deal(w4_codes[a][:], w4_raw[:, a, :], 2)
-            w1_q.append(quantise_weight("w1_%d" % a, w1_raw[a]))
+            w1_q.append(quantise_weight("w1_%d" % a, w1_raw[a], 64))
         v_w.append([gather_words(1, h) for h in range(2)])
+        w8_sc = sb("w8_sc", [P, H], U8)
+        nc.vector.tensor_copy(
+            w8_sc[:].rearrange("p (t a q) -> p t a q", t=PACK, a=2),
+            planes[:, :, S + H : S + H + H // 2].rearrange("p a (q t) -> p t a q", t=PACK),
+        )
+        w8_codes = sb("w8_codes", [P, H], I32)
+        deal(w8_codes[:], w8_raw[:], 1)
 
         diff = {}
 
@@ -216,11 +222,7 @@ def tile_list_inclusion_page_planes_kernel(
                     nc.vector.tensor_copy(part, page[t][:].indirect(list3[:, LIST_HALF * h : LIST_HALF * (h + 1)]))
                     scale_into_x(t, h, part)
 
-        w2_codes, w2_sc = quantise_weight("w2", w2_raw, "hval2")
-        w8_codes = sb("w8_codes", [P, H], I32, "hval1")
-        deal(w8_codes[:], w8_raw[:], 1)
-        w8_sc = sb("w8_sc", [P, H], U8, "wgs_1")
-        deal(w8_sc[:], w8_sc_raw[:], 1)
+        w2_codes, w2_sc = quantise_weight("w2", w2_raw, P, "hval2")
 
         x_q = []
         for h in range(2):
@@ -232,13 +234,15 @@ def tile_list_inclusion_page_planes_kernel(
             x_q.append((codes, scales))
 
         out_rows = out.rearrange("(p t) m -> p t m", t=PACK)
-        units = [(t, h) for h in range(2) for t in range(PACK - 1)] + [(PACK - 1, h) for h in range(2)]
-        first = [sb("first%d" % i, [P, M], F32) for i in range(PACK)]
-        gate = [hval[0], hval[3], work[0], first[0]]
+        units = [(t, h) for h in range(2) for t in range(PACK)]
+        first = [sb("first%d" % u, [P, HALF], F32) for u in range(len(units))]
+        gate = [hval[0][:, 0:HALF], hval[3][:, 0:HALF], hval[3][:, HALF:S], work[1][:, 0:HALF]]
+        gate.extend(first[u][:] for u in range(1, 5))
 
-        def mirror(t):
-            nc.vector.tensor_copy(gate[t][:], page[t][:].indirect(list4[:]))
-            nc.scalar.activation(gate[t][:], gate[t][:], ACT.Sigmoid, scale=mir_t[:, t : t + 1])
+        def mirror(u):
+            t, h = units[u]
+            nc.vector.tensor_copy(gate[u], page[t][:].indirect(list4[:, LIST_HALF * h : LIST_HALF * (h + 1)]))
+            nc.scalar.activation(gate[u], gate[u], ACT.Sigmoid, scale=mir_t[:, t : t + 1])
 
         def larger_side(u):
             t, h = units[u]
@@ -250,27 +254,21 @@ def tile_list_inclusion_page_planes_kernel(
                     out=y[:], lhsT=codes[:, cols].bitcast(FP8X4), lhsT_scale=scales[:, cols],
                     rhs=x_q[h][0][:].bitcast(FP8X4), rhs_scale=x_q[h][1][:], start=True, stop=True,
                 )
-            side = first[u // 2][:, HALF * (u % 2) : HALF * (u % 2 + 1)]
-            nc.scalar.copy(side, y1[:])
+            nc.scalar.copy(first[u][:], y1[:])
             larger = sb("larger%d" % u, [P, HALF], F32)
-            nc.vector.tensor_tensor(larger[:], y2[:], side, ALU.max)
+            nc.vector.tensor_tensor(larger[:], y2[:], first[u][:], ALU.max)
             return larger
 
-        def finish(u, larger):
+        def finish(u, larger, engine):
             t, h = units[u]
-            cols = slice(HALF * h, HALF * (h + 1))
-            engine = nc.gpsimd if t < PACK - 1 else nc.vector
-            engine.tensor_tensor(larger[:], larger[:], gate[t][:, cols], ALU.mult)
-            nc.sync.dma_start(out_rows[:, t, cols], larger[:])
+            engine.tensor_tensor(larger[:], larger[:], gate[u], ALU.mult)
+            nc.sync.dma_start(out_rows[:, t, HALF * h : HALF * (h + 1)], larger[:])
 
-        for t in range(PACK - 1):
-            mirror(t)
+        for u in range(PACK):
+            mirror(u)
         larger = []
         for u in range(len(units)):
             larger.append(larger_side(u))
-            if u == 2:
-                mirror(PACK - 1)
-            if u < len(units) - 2:
-                finish(u, larger[u])
-        for u in range(len(units) - 2, len(units)):
-            finish(u, larger[u])
+            if 1 <= u <= 4:
+                mirror(u + 3)
+            finish(u, larger[u], nc.gpsimd if u < len(units) - 1 else nc.vector)

@@ -51,9 +51,9 @@ def tile_list_inclusion_page_planes_kernel(
             nc.sync.dma_start(tile[SPARE:P, :].bitcast(I32), src.rearrange("a q c -> q a c").bitcast(I32))
             return tile
 
-        def load_vector(name, src):
+        def load_vector(name, src, queue):
             tile = sb(name, [P, PACK], F32)
-            nc.sync.dma_start(tile[:], src.rearrange("(p t) -> p t", t=PACK))
+            queue.dma_start(tile[:], src.rearrange("(p t) -> p t", t=PACK))
             return tile
 
         def load_table(a):
@@ -89,6 +89,7 @@ def tile_list_inclusion_page_planes_kernel(
             staged[SPARE:P, S + H : S + H + H // 2].bitcast(I32),
             w8_scales[0].rearrange("q (a c) -> (q a) c", a=2).bitcast(I32),
         )
+        gain_t = load_vector("gain_t", gain, nc.gpsimd)
         planes = sb("planes", [P, 2, S + H + H // 2], U8)
         nc.gpsimd.memset(planes[:].bitcast(I32), 0)
         tab = [load_table(0)]
@@ -96,32 +97,31 @@ def tile_list_inclusion_page_planes_kernel(
         nc.sync.dma_start(w4_raw[:].bitcast(I32), w4_words.rearrange("a p b -> p a b").bitcast(I32))
         w1_raw = [load_weight_rows("w1_raw%d" % a, w1[512 * a : 512 * (a + 1), :]) for a in range(2)]
         tab.append(load_table(1))
-        gain_t = load_vector("gain_t", gain)
+        list2 = load_list("list2", offs2)
         wgs_0a = load_wgs("wgs_0a", 0, HALF)
         w8_raw = sb("w8_raw", [P, H], I32)
         nc.sync.dma_start(w8_raw[:], w8_words[0].rearrange("p c i -> p (c i)").bitcast(I32))
         page = [load_page(0)]
-        list2 = load_list("list2", offs2)
         wgs_0b = load_wgs("wgs_0b", HALF, S)
         list3 = load_list("list3", offs3)
-        reach_t = load_vector("reach_t", reach)
+        reach_t = load_vector("reach_t", reach, nc.sync)
         page.append(load_page(1))
         wgs_1 = load_wgs("wgs_1", S, 2 * S)
         w2_raw = load_weight_rows("w2_raw", w2)
         list4 = load_list("list4", offs4)
-        mir_t = load_vector("mir_t", mir)
+        mir_t = load_vector("mir_t", mir, nc.sync)
         page.append(load_page(2))
         wgs_23 = load_wgs("wgs_23", 2 * S, 4 * S)
         page.append(load_page(3))
 
-        def quantise_weight(name, raw, scalar_share, tag=None):
-            grouped = sb(name + "_bf", [P, PACK, P, PACK], BF16)
+        def quantise_weight(name, raw, scalar_share, grouped_tag, codes_tag):
+            grouped = sb(name + "_bf", [P, PACK, P, PACK], BF16, grouped_tag)
             dst = grouped[:].rearrange("p t q j -> p q t j")
             src = raw[:].rearrange("p j (q t) -> p q t j", t=PACK)
             nc.scalar.copy(dst[:, 0:scalar_share], src[:, 0:scalar_share])
             if scalar_share < P:
                 nc.vector.tensor_copy(dst[:, scalar_share:P], src[:, scalar_share:P])
-            codes = sb(name + "_codes", [P, H], U32, tag)
+            codes = sb(name + "_codes", [P, H], U32, codes_tag)
             scales = sb(name + "_scales", [P, H], U8)
             nc.vector.quantize_mx(
                 out=codes[:].bitcast(FP8X4), scales=scales[:],
@@ -156,15 +156,16 @@ def tile_list_inclusion_page_planes_kernel(
         w1_q = []
         for a in range(2):
             deal(w4_codes[a][:], w4_raw[:, a, :], 2)
-            w1_q.append(quantise_weight("w1_%d" % a, w1_raw[a], 64))
+            w1_q.append(quantise_weight("w1_%d" % a, w1_raw[a], 64, ("tab0", "w1_raw0")[a], None))
         v_w.append([gather_words(1, h) for h in range(2)])
-        w8_sc = sb("w8_sc", [P, H], U8)
+        w8_dealt = sb("w8_dealt", [P, 5 * H], U8, "tab1")
+        w8_codes = w8_dealt[:, 0 : 4 * H].bitcast(I32)
+        w8_sc = w8_dealt[:, 4 * H : 5 * H]
         nc.vector.tensor_copy(
-            w8_sc[:].rearrange("p (t a q) -> p t a q", t=PACK, a=2),
+            w8_sc.rearrange("p (t a q) -> p t a q", t=PACK, a=2),
             planes[:, :, S + H : S + H + H // 2].rearrange("p a (q t) -> p t a q", t=PACK),
         )
-        w8_codes = sb("w8_codes", [P, H], I32)
-        deal(w8_codes[:], w8_raw[:], 1)
+        deal(w8_codes, w8_raw[:], 1)
 
         diff = {}
 
@@ -222,7 +223,7 @@ def tile_list_inclusion_page_planes_kernel(
                     nc.vector.tensor_copy(part, page[t][:].indirect(list3[:, LIST_HALF * h : LIST_HALF * (h + 1)]))
                     scale_into_x(t, h, part)
 
-        w2_codes, w2_sc = quantise_weight("w2", w2_raw, P, "hval2")
+        w2_codes, w2_sc = quantise_weight("w2", w2_raw, P, None, "hval2")
 
         x_q = []
         for h in range(2):

from contextlib import ExitStack

import concourse.mybir as mybir

K, H, T, S, T2, M = 1024, 512, 4096, 1024, 2048, 1024
FLOPS = 2 * (2 * K * H * S + 2 * H * H * M)

F32 = mybir.dt.float32
BF16 = mybir.dt.bfloat16
I32 = mybir.dt.int32
U32 = mybir.dt.uint32
U16 = mybir.dt.uint16
U8 = mybir.dt.uint8
FP8X4 = mybir.dt.float8_e4m3fn_x4
FP4X4 = mybir.dt.float4_e2m1fn_x4
ACT = mybir.ActivationFunctionType
ALU = mybir.AluOpType

P = 128
PACK = 4
QUADS = 4
HALF = 512
LIST_HALF = HALF // 16
SPARE = 96


def tile_list_inclusion_page_planes_kernel(
    tc, tab_words, tab_scales, offs, offs2, offs3, offs4, w1, w4_words, w4_scales,
    gain, wgs, page0, reach, w2, w8_words, w8_scales, mir, out,
):
    nc = tc.nc
    with ExitStack() as ctx:
        keep = ctx.enter_context(tc.tile_pool(name="keep", bufs=1))
        ring = ctx.enter_context(tc.tile_pool(name="ring", bufs=2))
        psum = ctx.enter_context(tc.psum_pool(name="psum", bufs=1))

        def sb(name, shape, dtype, tag=None):
            return keep.tile(shape, dtype, name=name, tag=tag or name, align_bytes=64)

        def bank(b):
            return psum.tile([P, HALF], F32, name="bank%d" % b)

        def load_list(name, src):
            tile = keep.tile([P, S // 16], U16, name=name)
            nc.sync.dma_start(tile[:], src)
            return tile

        def load_scale_rows(name, src, width, clear):
            tile = sb(name, [P, width], U8)
            clear(tile[0:SPARE, :].bitcast(I32), 0)
            nc.sync.dma_start(tile[SPARE:P, :].bitcast(I32), src.rearrange("a q c -> q a c").bitcast(I32))
            return tile

        def load_vector(name, src, queue):
            tile = sb(name, [P, PACK], F32)
            queue.dma_start(tile[:], src.rearrange("(p t) -> p t", t=PACK))
            return tile

        def load_table(a):
            tile = sb("tab%d" % a, [P, T], I32)
            nc.sync.dma_start(tile[:], tab_words[a].rearrange("p c i -> p (c i)").bitcast(I32))
            return tile

        def load_weight_rows(name, rows):
            tile = sb(name, [P, PACK, H], F32)
            nc.sync.dma_start(tile[:], rows.rearrange("(p j) c -> p j c", j=PACK))
            return tile

        wgs_rows = wgs.rearrange("(p t) j -> p (t j)", t=PACK)

        def load_wgs(name, lo, hi):
            tile = sb(name, [P, hi - lo], F32)
            for q in (0, 2, 1, 3):
                nc.sync.dma_start(tile[32 * q : 32 * q + 32, :], wgs_rows[:, lo:hi])
            return tile

        page_rows = page0.rearrange("(p t) c -> p t c", t=PACK)

        def load_page(t):
            tile = sb("page%d" % t, [P, T2], F32)
            nc.sync.dma_start(tile[:], page_rows[:, t, :])
            return tile

        list1 = load_list("list1", offs)
        tab_sc = load_scale_rows("tab_sc", tab_scales, T, nc.vector.memset)
        w4_sc_raw = load_scale_rows("w4_sc_raw", w4_scales, H, nc.vector.memset)
        staged = sb("staged", [P, S + H + H // 2], U8)
        nc.sync.dma_start(
            staged[SPARE:P, S + H : S + H + H // 2].bitcast(I32),
            w8_scales[0].rearrange("q (a c) -> (q a) c", a=2).bitcast(I32),
        )
        gain_t = load_vector("gain_t", gain, nc.gpsimd)
        planes = sb("planes", [P, 2, S + H + H // 2], U8)
        nc.gpsimd.memset(planes[:].bitcast(I32), 0)
        tab = [load_table(0)]
        w4_raw = sb("w4_raw", [P, 2, 2 * H], U8)
        nc.sync.dma_start(w4_raw[:].bitcast(I32), w4_words.rearrange("a p b -> p a b").bitcast(I32))
        w1_raw = [load_weight_rows("w1_raw%d" % a, w1[512 * a : 512 * (a + 1), :]) for a in range(2)]
        tab.append(load_table(1))
        list2 = load_list("list2", offs2)
        wgs_0a = load_wgs("wgs_0a", 0, HALF)
        w8_raw = sb("w8_raw", [P, H], I32)
        nc.sync.dma_start(w8_raw[:], w8_words[0].rearrange("p c i -> p (c i)").bitcast(I32))
        page = [load_page(0)]
        wgs_0b = load_wgs("wgs_0b", HALF, S)
        list3 = load_list("list3", offs3)
        reach_t = load_vector("reach_t", reach, nc.sync)
        page.append(load_page(1))
        wgs_1 = load_wgs("wgs_1", S, 2 * S)
        w2_raw = load_weight_rows("w2_raw", w2)
        list4 = load_list("list4", offs4)
        mir_t = load_vector("mir_t", mir, nc.sync)
        page.append(load_page(2))
        wgs_23 = load_wgs("wgs_23", 2 * S, 4 * S)
        page.append(load_page(3))

        def quantise_weight(name, raw, scalar_share, grouped_tag, codes_tag):
            grouped = sb(name + "_bf", [P, PACK, P, PACK], BF16, grouped_tag)
            dst = grouped[:].rearrange("p t q j -> p q t j")
            src = raw[:].rearrange("p j (q t) -> p q t j", t=PACK)
            nc.scalar.copy(dst[:, 0:scalar_share], src[:, 0:scalar_share])
            if scalar_share < P:
                nc.vector.tensor_copy(dst[:, scalar_share:P], src[:, scalar_share:P])
            codes = sb(name + "_codes", [P, H], U32, codes_tag)
            scales = sb(name + "_scales", [P, H], U8)
            nc.vector.quantize_mx(
                out=codes[:].bitcast(FP8X4), scales=scales[:],
                in_=grouped[:].rearrange("p t q j -> p (t q j)"),
            )
            return codes, scales

        def deal(dst, raw, unit):
            nc.vector.tensor_copy(
                dst.rearrange("p (t q b) -> p t q b", t=PACK, b=unit),
                raw.rearrange("p (q t b) -> p t q b", t=PACK, b=unit),
            )

        def gather_words(a, h):
            tile = sb("v_w%d_%d" % (a, h), [P, HALF], U32)
            nc.vector.tensor_copy(
                tile[:], tab[a][:].bitcast(U32).indirect(list1[:, LIST_HALF * h : LIST_HALF * (h + 1)])
            )
            return tile

        deal(staged[:, S : S + H], w4_sc_raw[:], 1)
        picked_sc = sb("picked_sc", [P, S], U8)
        nc.vector.tensor_copy(picked_sc[:], tab_sc[:].indirect(list1[:]))
        nc.vector.tensor_copy(staged[:, 0:S].bitcast(I32), picked_sc[:].bitcast(I32))
        for q in range(QUADS):
            nc.gpsimd.dma_start(
                planes[32 * q : 32 * q + 4, :, :].bitcast(I32),
                staged[SPARE + 8 * q : SPARE + 8 * q + 8, :].bitcast(I32),
            )
        v_w = [[gather_words(0, h) for h in range(2)]]
        w4_codes = [sb("w4_codes%d" % a, [P, 2 * H], U8) for a in range(2)]
        w1_q = []
        for a in range(2):
            deal(w4_codes[a][:], w4_raw[:, a, :], 2)
            w1_q.append(quantise_weight("w1_%d" % a, w1_raw[a], 64, ("tab0", "w1_raw0")[a], None))
        v_w.append([gather_words(1, h) for h in range(2)])
        w8_dealt = sb("w8_dealt", [P, 5 * H], U8, "tab1")
        w8_codes = w8_dealt[:, 0 : 4 * H].bitcast(I32)
        w8_sc = w8_dealt[:, 4 * H : 5 * H]
        nc.vector.tensor_copy(
            w8_sc.rearrange("p (t a q) -> p t a q", t=PACK, a=2),
            planes[:, :, S + H : S + H + H // 2].rearrange("p a (q t) -> p t a q", t=PACK),
        )
        deal(w8_codes, w8_raw[:], 1)

        diff = {}

        def diff_passes(a, t, h):
            cols = slice(P * t, P * (t + 1))
            rhs = v_w[a][h][:].bitcast(FP8X4)
            rhs_scale = planes[:, a, HALF * h : HALF * (h + 1)]
            nc.tensor.matmul_mx(
                out=diff[t, h][:],
                lhsT=w4_codes[a][:, 2 * P * t : 2 * P * (t + 1)].bitcast(FP4X4), lhsT_scale=planes[:, a, S + P * t : S + P * (t + 1)],
                rhs=rhs, rhs_scale=rhs_scale, start=(a == 0), stop=False,
            )
            nc.tensor.matmul_mx(
                out=diff[t, h][:],
                lhsT=w1_q[a][0][:, cols].bitcast(FP8X4), lhsT_scale=w1_q[a][1][:, cols],
                rhs=rhs, rhs_scale=rhs_scale, start=False, stop=(a == 1),
            )

        work = [sb("work%d" % h, [P, S], F32) for h in range(2)]
        x_bf = [work[h][:].bitcast(BF16) for h in range(2)]
        hval = [sb("hval%d" % t, [P, S], F32) for t in range(PACK)]
        for t in range(PACK):
            for h in range(2):
                diff[t, h] = bank(h)
                diff_passes(0, t, h)
                diff_passes(1, t, h)
                part = hval[t][:, HALF * h : HALF * (h + 1)]
                squared = work[1 - h][:, 0:HALF]
                nc.scalar.activation(squared, diff[t, h][:], ACT.Square)
                nc.scalar.activation(part, squared, ACT.Copy, scale=gain_t[:, t : t + 1])


        def put(t, entries, values, weights):
            nc.vector.tensor_tensor(page[t][:].indirect(entries), values, weights, ALU.mult)

        def scale_into_x(t, h, picked):
            nc.scalar.activation(x_bf[h][:, t : PACK * HALF : PACK], picked, ACT.Copy, scale=reach_t[:, t : t + 1])

        for t in range(PACK):
            if t == 0:
                put(0, list2[:, 0:LIST_HALF], hval[0][:, 0:HALF], wgs_0a[:])
                put(0, list2[:, LIST_HALF : 2 * LIST_HALF], hval[0][:, HALF:S], wgs_0b[:])
            elif t == 1:
                put(1, list2[:], hval[1][:], wgs_1[:])
            else:
                put(t, list2[:], hval[t][:], wgs_23[:, S * (t - 2) : S * (t - 1)])
            picked = ring.tile([P, M], F32, name="picked", align_bytes=64)
            if t < PACK - 1:
                nc.vector.tensor_copy(picked[:], page[t][:].indirect(list3[:]))
                for h in range(2):
                    scale_into_x(t, h, picked[:, HALF * h : HALF * (h + 1)])
            else:
                for h in range(2):
                    part = picked[:, HALF * h : HALF * (h + 1)]
                    nc.vector.tensor_copy(part, page[t][:].indirect(list3[:, LIST_HALF * h : LIST_HALF * (h + 1)]))
                    scale_into_x(t, h, part)

        w2_codes, w2_sc = quantise_weight("w2", w2_raw, P, None, "hval2")

        x_q = []
        for h in range(2):
            codes = sb("x_codes%d" % h, [P, HALF], U32)
            scales = sb("x_scales%d" % h, [P, HALF], U8)
            nc.vector.quantize_mx(
                out=codes[:].bitcast(FP8X4), scales=scales[:], in_=x_bf[h]
            )
            x_q.append((codes, scales))

        out_rows = out.rearrange("(p t) m -> p t m", t=PACK)
        units = [(t, h) for h in range(2) for t in range(PACK)]
        first = [sb("first%d" % u, [P, HALF], F32) for u in range(len(units))]
        gate = [hval[0][:, 0:HALF], hval[3][:, 0:HALF], hval[3][:, HALF:S], work[1][:, 0:HALF]]
        gate.extend(first[u][:] for u in range(1, 5))

        def mirror(u):
            t, h = units[u]
            nc.vector.tensor_copy(gate[u], page[t][:].indirect(list4[:, LIST_HALF * h : LIST_HALF * (h + 1)]))
            nc.scalar.activation(gate[u], gate[u], ACT.Sigmoid, scale=mir_t[:, t : t + 1])

        def larger_side(u):
            t, h = units[u]
            cols = slice(P * t, P * (t + 1))
            y1 = bank((2 * u) % 8)
            y2 = bank((2 * u + 1) % 8)
            for y, codes, scales in ((y1, w2_codes, w2_sc), (y2, w8_codes, w8_sc)):
                nc.tensor.matmul_mx(
                    out=y[:], lhsT=codes[:, cols].bitcast(FP8X4), lhsT_scale=scales[:, cols],
                    rhs=x_q[h][0][:].bitcast(FP8X4), rhs_scale=x_q[h][1][:], start=True, stop=True,
                )
            nc.scalar.copy(first[u][:], y1[:])
            larger = sb("larger%d" % u, [P, HALF], F32)
            nc.vector.tensor_tensor(larger[:], y2[:], first[u][:], ALU.max)
            return larger

        def finish(u, larger, engine):
            t, h = units[u]
            engine.tensor_tensor(larger[:], larger[:], gate[u], ALU.mult)
            nc.sync.dma_start(out_rows[:, t, HALF * h : HALF * (h + 1)], larger[:])

        for u in range(PACK):
            mirror(u)
        larger = []
        for u in range(len(units)):
            larger.append(larger_side(u))
            if 1 <= u <= 4:
                mirror(u + 3)
            finish(u, larger[u], nc.gpsimd if u < len(units) - 1 else nc.vector)
